import numpy as np
import ml_dtypes


def mxq(x, axis, fmt="e4m3"):
    dtype, down = {"e4m3": (ml_dtypes.float8_e4m3fn, 7), "e5m2": (ml_dtypes.float8_e5m2, 14)}[fmt]
    v = np.moveaxis(np.asarray(x, np.float32).astype(ml_dtypes.bfloat16).astype(np.float64), axis, -1)
    blocks = v.reshape(v.shape[:-1] + (-1, 32))
    amax = np.abs(blocks).max(-1, keepdims=True)
    byte = np.maximum(np.where(amax > 0, np.frexp(amax)[1] - 1 + 127, 0) - down, 1)
    scale = np.exp2(byte - 127.0)
    codes = (blocks / scale).astype(np.float32).astype(dtype).astype(np.float64)
    return np.moveaxis((codes * scale).reshape(v.shape), -1, axis)


WIDE = False


def mx_kscale(k):
    if not WIDE:
        return np.ones(k)
    levels = np.array([10, -10, 5, -5, 0])
    if k % 512:
        return np.exp2(np.random.permutation(np.resize(levels, k // 32))).repeat(32)
    a = np.empty((k // 512, 16))
    for p in range(k // 512):
        a[p, :8] = np.random.permutation(np.resize(levels, 8))
        for g in range(8):
            far = levels[np.abs(levels - a[p, g]) >= 10]
            a[p, g + 8] = far[np.random.randint(len(far))]
    return np.exp2(a.ravel()).repeat(32)


def f64(x):
    return np.asarray(x).astype(np.float64)


def striped(idx):
    return np.tile(idx.reshape(-1, 16).T, (8, 1)).astype(np.uint16)


def unstriped(offs):
    return offs[:16].T.reshape(-1).astype(np.int64)


E2M1 = np.array([0.0, 0.5, 1.0, 1.5, 2.0, 3.0, 4.0, 6.0, -0.0, -0.5, -1.0, -1.5, -2.0, -3.0, -4.0, -6.0])


def pack_weight(w, fmt):
    k, n = w.shape
    w = f64(np.asarray(w, np.float32).astype(ml_dtypes.bfloat16)).reshape(k // 32, 32, n)
    amax = np.abs(w).max(1)
    if fmt == "e4m3":
        byte = np.frexp(amax)[1] - 1 + 127 - 7
    else:
        mant, ex = np.frexp(amax / 6.0)
        byte = np.where(mant > 0.5, ex, ex - 1) + 127
    byte = np.clip(np.where(amax > 0, byte, 1), 1, 254)
    scaled = (w * np.exp2(127.0 - byte)[:, None, :]).reshape(k, n).astype(np.float32)
    by_word = np.ascontiguousarray(scaled.reshape(k // 512, 128, 4, n).transpose(0, 1, 3, 2))
    if fmt == "e4m3":
        words = by_word.astype(ml_dtypes.float8_e4m3fn).view(np.uint8)
    else:
        c = by_word.astype(ml_dtypes.float4_e2m1fn).view(np.uint8) & 0xF
        words = (c[..., 0::2] | (c[..., 1::2] << 4)).reshape(k // 512, 128, 2 * n)
    return np.ascontiguousarray(words), np.ascontiguousarray(byte.astype(np.uint8).reshape(k // 512, 16, n))


def unpack_weight(words, scales, fmt):
    g, _, n = scales.shape
    words = np.ascontiguousarray(words).reshape(g, 128, n, -1)
    if fmt == "e4m3":
        vals = words.view(ml_dtypes.float8_e4m3fn).astype(np.float64)
    else:
        nib = np.empty((g, 128, n, 4), np.uint8)
        nib[..., 0::2] = words & 0xF
        nib[..., 1::2] = words >> 4
        vals = E2M1[nib]
    vals = vals * np.repeat(np.exp2(scales.astype(np.float64) - 127.0), 8, axis=1)[..., None]
    return vals.transpose(0, 1, 3, 2).reshape(g * 512, n)


def gelu(v):
    return 0.5 * v * (1.0 + np.tanh(np.sqrt(2.0 / np.pi) * (v + 0.044715 * v**3)))


def striped8(idx):
    return np.concatenate([v.reshape(-1, 16).T for v in idx]).astype(np.uint16)


def unstriped8(offs):
    return np.stack([offs[16 * g:16 * g + 16].T.reshape(-1) for g in range(8)]).astype(np.int64)


def runs(v, idx8):
    k = np.arange(v.shape[0])
    return v[k[:, None], idx8[k % 512 // 64]]


K, T, S, P, H, N = 1536, 2048, 1024, 512, 1024, 768

def setup_inputs():
    n = np.random.standard_normal
    s = mx_kscale(K)[:, None]
    u = mx_kscale(H)[:, None]
    d = {}
    d["tab_words"], d["tab_scales"] = pack_weight(n((K, T)) * s, "e4m3")
    d["offs"] = striped8(np.stack([np.random.permutation(T)[:S] for _ in range(8)]))
    d["pos1"] = striped(np.random.permutation(S)[:P])
    d["pos2"] = striped(np.random.permutation(S)[:P])
    d["w1"] = (n((K, H)) / K**0.5 / s).astype(np.float32)
    d["gain"] = (np.exp(0.3 * n(H)) * u[:, 0]).astype(np.float32)
    d["w4_words"], d["w4_scales"] = pack_weight(0.8 * n((H, N)) / H**0.5 / u, "e2m1")
    d["bias"] = (0.7 * n(N)).astype(np.float32)
    return d

def reference(tab_words, tab_scales, offs, pos1, pos2, w1, gain, w4_words, w4_scales, bias):
    v = runs(unpack_weight(tab_words, tab_scales, "e4m3"), unstriped8(offs))
    h = f64(gain)[:, None] * (mxq(f64(w1), 0, "e4m3").T @ v)
    rag = np.abs(h[:, unstriped(pos1)] - h[:, unstriped(pos2)])
    w4 = unpack_weight(w4_words, w4_scales, "e2m1")
    y = w4.T @ mxq(rag, 0, "e4m3")
    return np.tanh(y + f64(bias)[:, None])

@@ -1,0 +1,260 @@
+from contextlib import ExitStack
+
+import concourse.mybir as mybir
+
+K, T, S, NP, H, N = 1536, 2048, 1024, 512, 1024, 768
+FLOPS = 2 * K * H * S + 2 * H * N * NP
+
+F32 = mybir.dt.float32
+BF16 = mybir.dt.bfloat16
+I32 = mybir.dt.int32
+U32 = mybir.dt.uint32
+U16 = mybir.dt.uint16
+U8 = mybir.dt.uint8
+FP8X4 = mybir.dt.float8_e4m3fn_x4
+FP4X4 = mybir.dt.float4_e2m1fn_x4
+ACT = mybir.ActivationFunctionType
+ALU = mybir.AluOpType
+
+P = 128
+PLANE = (0, 8, 4)
+REUSE = {(0, 2, 0): "grp12", (0, 3, 0): "grp11", (1, 0, 256): "vw1", (1, 2, 256): "rb0", (1, 2, 384): "rb256"}
+CHUNKS = ((0, 256), (256, 128), (384, 128))
+
+
+def tile_list_heave_raggedness_scores_kernel(
+    tc, tab_words, tab_scales, offs, pos1, pos2, w1, gain, w4_words, w4_scales, bias, out
+):
+    nc = tc.nc
+    with ExitStack() as ctx:
+        lists = ctx.enter_context(tc.tile_pool(name="lists", bufs=1))
+        keep = ctx.enter_context(tc.tile_pool(name="keep", bufs=1))
+        ring = ctx.enter_context(tc.tile_pool(name="ring", bufs=5))
+        work = ctx.enter_context(tc.tile_pool(name="work", bufs=3))
+        psum = ctx.enter_context(tc.psum_pool(name="psum", bufs=8))
+
+        offs_t = lists.tile([P, S // 16], U16, name="offs_t")
+        pos1_t = lists.tile([P, NP // 16], U16, name="pos1_t")
+        pos2_t = lists.tile([P, NP // 16], U16, name="pos2_t")
+        nc.sync.dma_start(offs_t[:], offs)
+
+        sw = ring.tile([P, T], U8, tag="ring", name="sw", align_bytes=64)
+        nc.vector.memset(sw[:].bitcast(I32), 0)
+        by_r = tab_scales.rearrange("a (g r) t -> r g a t", r=2)
+        for r in range(2):
+            nc.sync.dma_start(sw[r:P:8, :].bitcast(I32), by_r[r, :, 0:2, :].bitcast(I32))
+            nc.sync.dma_start(sw[4 + r : P : 16, :].bitcast(I32), by_r[r, :, 2, :].bitcast(I32))
+
+        nc.sync.dma_start(pos1_t[:], pos1)
+        nc.sync.dma_start(pos2_t[:], pos2)
+        warm_in = keep.tile([P, 8], F32, name="warm_in")
+        warm_out = keep.tile([P, 8], F32, name="warm_out")
+        nc.gpsimd.memset(warm_in[:], 0.0)
+        nc.scalar.activation(warm_out[:], warm_in[:], ACT.Tanh)
+
+        gain_t = keep.tile([P, 2, 4], F32, name="gain_t")
+        w4s = keep.tile([P, 2, N], U8, name="w4s", align_bytes=64)
+        nc.gpsimd.dma_start(gain_t[:], gain.rearrange("(b p t) -> p b t", b=2, t=4))
+        nc.gpsimd.memset(w4s[:].rearrange("p a n -> p (a n)").bitcast(I32), 0)
+        w4s_by_r = w4_scales.rearrange("a (q r) n -> r q a n", r=4)
+        for r in range(4):
+            nc.gpsimd.dma_start(w4s[r:P:32, :, :].bitcast(I32), w4s_by_r[r].bitcast(I32))
+
+        def load_tab(a):
+            tab = ring.tile([P, T], U32, tag="ring", name="tab%d" % a, align_bytes=64)
+            nc.sync.dma_start(tab[:].bitcast(I32), tab_words[a].rearrange("p t i -> p (t i)").bitcast(I32))
+            return tab
+
+        def load_w1(b, a, c0, width):
+            raw = ring.tile([P, 4, width], F32, tag="ring", name="raw%d%d%d" % (b, a, c0), align_bytes=64)
+            rows = w1[512 * a : 512 * (a + 1), 512 * b + c0 : 512 * b + c0 + width]
+            nc.sync.dma_start(raw[:], rows.rearrange("(p j) c -> p j c", j=4))
+            return raw
+
+        def cast_w1(engine_copy, grouped, raw, c0, width):
+            dst = grouped[:].rearrange("p (t m j) -> p m j t", t=4, j=4)[:, c0 // 4 : (c0 + width) // 4]
+            engine_copy(dst, raw.rearrange("p j (m t) -> p m j t", t=4))
+
+        w1q = {}
+
+        def quantize_w1(b, a, grouped, parts):
+            codes = keep.tile([P, 512], U32, name="w1c%d%d" % (b, a), align_bytes=64)
+            scales = keep.tile([P, 512], U8, name="w1s%d%d" % (b, a), align_bytes=64)
+            step = 512 // parts
+            for c in range(0, 512, step):
+                nc.vector.quantize_mx(
+                    out=codes[:, c : c + step].bitcast(FP8X4),
+                    scales=scales[:, c : c + step],
+                    in_=grouped[:, 4 * c : 4 * (c + step)],
+                )
+            w1q[(b, a)] = (codes, scales)
+
+        def new_grouped(b, a):
+            return keep.tile([P, 2048], BF16, tag="grp%d%d" % (b, a), name="grp%d%d" % (b, a), align_bytes=64)
+
+        tabs = [load_tab(0)]
+        raw00 = load_w1(0, 0, 0, 512)
+        tabs.extend([load_tab(1), load_tab(2)])
+        g00, g01, g02 = new_grouped(0, 0), new_grouped(0, 1), new_grouped(0, 2)
+        cast_w1(nc.scalar.copy, g00, raw00[:], 0, 512)
+
+        vw = []
+        sg = keep.tile([P, S], U8, name="sg", align_bytes=64)
+        sf = keep.tile([P, S], U8, name="sf", align_bytes=64)
+        for a in range(3):
+            v = keep.tile([P, S], U32, tag="vw%d" % a, name="vw%d" % a, align_bytes=64)
+            if a == 0:
+                nc.vector.tensor_copy(sg[:], sw[:].indirect(offs_t[:]))
+                nc.vector.tensor_copy(sf[:].bitcast(I32), sg[:].bitcast(I32))
+                for r in range(2):
+                    nc.sync.dma_start(
+                        sf[2 + r : 2 + r + 109 : 4, :].bitcast(I32), sg[16 + r : 16 + r + 109 : 4, :].bitcast(I32)
+                    )
+            nc.vector.tensor_copy(v[:], tabs[a][:].indirect(offs_t[:]))
+            vw.append(v)
+            if a == 1:
+                quantize_w1(0, 0, g00, 1)
+
+        raw01 = load_w1(0, 1, 0, 512)
+        raw02 = [load_w1(0, 2, c0, 256) for c0 in (0, 256)]
+        raw1 = [load_w1(1, a, 0, 512) for a in range(3)]
+        w4w = ring.tile([P, 2, 2 * N], U8, tag="ring", name="w4w", align_bytes=64)
+        nc.sync.dma_start(w4w[:].bitcast(I32), w4_words.rearrange("a p n -> p a n").bitcast(I32))
+
+        bias_t = ring.tile([P, 6], F32, tag="ring", name="bias_t", align_bytes=64)
+        with nc.allow_non_contiguous_dma(reason="one bias value a partition"):
+            nc.sync.dma_start(bias_t[:], bias.rearrange("(c p) -> p c", p=P))
+
+        cast_w1(nc.scalar.copy, g01, raw01[:, :, 0:256], 0, 256)
+        cast_w1(nc.vector.tensor_copy, g01, raw01[:, :, 256:512], 256, 256)
+        cast_w1(nc.scalar.copy, g02, raw02[0][:], 0, 256)
+        quantize_w1(0, 1, g01, 1)
+        cast_w1(nc.vector.tensor_copy, g02, raw02[1][:], 256, 256)
+        quantize_w1(0, 2, g02, 2)
+
+        banks = {}
+
+        def first_product(b, a, t, last):
+            codes, scales = w1q[(b, a)]
+            for half in range(2):
+                if a == 0:
+                    banks[(b, t, half)] = psum.tile([P, 512], F32, tag="bank", name="hb%d%d%d" % (b, t, half))
+                cols = slice(512 * half, 512 * (half + 1))
+                nc.tensor.matmul_mx(
+                    out=banks[(b, t, half)][:],
+                    lhsT=codes[:, 128 * t : 128 * (t + 1)].bitcast(FP8X4),
+                    lhsT_scale=scales[:, 128 * t : 128 * (t + 1)],
+                    rhs=vw[a][:, cols].bitcast(FP8X4),
+                    rhs_scale=sf[PLANE[a] : P, cols],
+                    start=(a == 0),
+                    stop=(a == last),
+                )
+
+        h = {}
+
+        def evacuate(b, t):
+            h[(b, t)] = keep.tile([P, S], F32, name="h%d%d" % (b, t))
+            for half in range(2):
+                dst = h[(b, t)][:, 512 * half : 512 * (half + 1)]
+                if (b, t, half) == (0, 0, 1):
+                    nc.vector.tensor_scalar(dst, banks[(b, t, half)][:], gain_t[:, b, t : t + 1], None, ALU.mult)
+                else:
+                    nc.scalar.activation(dst, banks[(b, t, half)][:], ACT.Copy, scale=gain_t[:, b, t : t + 1])
+
+        def clock(src, name):
+            probe = keep.tile([P, 1], F32, name=name)
+            nc.gpsimd.tensor_copy(probe[:], src)
+
+        def pick_second(b, t, m0, width):
+            name = "sec%d%d%d" % (b, t, m0)
+            if (b, t, m0) in REUSE:
+                second = keep.tile([P, width], F32, tag=REUSE[(b, t, m0)], name=name, align_bytes=64)
+            else:
+                second = work.tile([P, width], F32, tag="second", name=name)
+            nc.vector.tensor_copy(second[:], h[(b, t)][:].indirect(pos2_t[:, m0 // 16 : (m0 + width) // 16]))
+            return second
+
+        def subtract(diff, second, b, t, m0, width):
+            nc.vector.tensor_tensor(
+                diff[:, t, :], h[(b, t)][:].indirect(pos1_t[:, m0 // 16 : (m0 + width) // 16]), second[:], ALU.subtract
+            )
+
+        def quantize_rag(diff, b, m0, width):
+            tag = "vw1" if b == 0 else "rb%d" % m0
+            rb = keep.tile([P, 4 * width], BF16, tag=tag, name="rb%d%d" % (b, m0), align_bytes=64)
+            nc.scalar.activation(
+                rb[:].rearrange("p (c i t) -> p c t i", i=4, t=4),
+                diff[:].rearrange("p t (c i) -> p c t i", i=4),
+                ACT.Abs,
+            )
+            codes = keep.tile([P, width], U32, name="rc%d%d" % (b, m0), align_bytes=64)
+            scales = keep.tile([P, width], U8, name="rs%d%d" % (b, m0), align_bytes=64)
+            nc.vector.quantize_mx(out=codes[:].bitcast(FP8X4), scales=scales[:], in_=rb[:])
+            return codes, scales
+
+        for t in range(4):
+            for a in range(3):
+                first_product(0, a, t, 2)
+
+        g1 = [new_grouped(1, a) for a in range(3)]
+        diff0 = keep.tile([P, 4, NP], F32, name="diff0")
+        for t in range(3):
+            evacuate(0, t)
+        cast_w1(nc.scalar.copy, g1[0], raw1[0][:], 0, 512)
+        cast_w1(nc.scalar.copy, g1[1], raw1[1][:], 0, 512)
+        evacuate(0, 3)
+        clock(h[(0, 0)][:, 0:1], "clk1")
+        seconds = [pick_second(0, t, 0, NP) for t in (0, 1)]
+        for t in range(2):
+            subtract(diff0, seconds[t], 0, t, 0, NP)
+        cast_w1(nc.vector.tensor_copy, g1[2], raw1[2][:], 0, 512)
+        quantize_w1(1, 0, g1[0], 1)
+        quantize_w1(1, 2, g1[2], 1)
+        second = pick_second(0, 2, 0, NP)
+        quantize_w1(1, 1, g1[1], 1)
+        subtract(diff0, second, 0, 2, 0, NP)
+        second = pick_second(0, 3, 0, NP)
+        subtract(diff0, second, 0, 3, 0, NP)
+        for t in range(4):
+            for a in (0, 2, 1):
+                first_product(1, a, t, 1)
+            evacuate(1, t)
+
+        clock(h[(1, 0)][:, 1023:1024], "clk2")
+        out_v = out.rearrange("(c p) m -> p c m", p=P)
+        rag = {}
+
+        def pick_chunk(m0, width):
+            diff = keep.tile([P, 4, width], F32, name="diff1%d" % m0)
+            for pair in range(2):
+                seconds = [pick_second(1, t, m0, width) for t in (2 * pair, 2 * pair + 1)]
+                for u in range(2):
+                    subtract(diff, seconds[u], 1, 2 * pair + u, m0, width)
+            if m0 == 0:
+                rag[0] = quantize_rag(diff0, 0, 0, NP)
+            rag[(1, m0)] = quantize_rag(diff, 1, m0, width)
+
+        def finish_chunk(m0, width):
+            y = keep.tile([P, 6, width], F32, name="y%d" % m0)
+            for c in range(6):
+                bank = psum.tile([P, 512], F32, tag="bank", name="yb%d%d" % (m0, c))
+                for s0 in range(0, width, 128):
+                    for a, (codes, scales, c0) in enumerate((rag[0] + (m0 + s0,), rag[(1, m0)] + (s0,))):
+                        nc.tensor.matmul_mx(
+                            out=bank[:, s0 : s0 + 128],
+                            lhsT=w4w[:, a, 256 * c : 256 * (c + 1)].bitcast(FP4X4),
+                            lhsT_scale=w4s[:, a, 128 * c : 128 * (c + 1)],
+                            rhs=codes[:, c0 : c0 + 128].bitcast(FP8X4),
+                            rhs_scale=scales[:, c0 : c0 + 128],
+                            start=(a == 0),
+                            stop=(a == 1),
+                        )
+                nc.scalar.activation(y[:, c, :], bank[:, 0:width], ACT.Tanh, bias=bias_t[:, c : c + 1])
+            for c0 in (0, 3):
+                nc.sync.dma_start(out_v[:, c0 : c0 + 3, m0 : m0 + width], y[:, c0 : c0 + 3, :])
+
+        pick_chunk(*CHUNKS[0])
+        for k in range(1, len(CHUNKS)):
+            pick_chunk(*CHUNKS[k])
+            finish_chunk(*CHUNKS[k - 1])
+        finish_chunk(*CHUNKS[-1])

@@ -18,7 +18,6 @@ ALU = mybir.AluOpType
 
 P = 128
 PLANE = (0, 8, 4)
-REUSE = {(0, 2, 0): "grp12", (0, 3, 0): "grp11", (1, 0, 256): "vw1", (1, 2, 256): "rb0", (1, 2, 384): "rb256"}
 CHUNKS = ((0, 256), (256, 128), (384, 128))
 
 
@@ -30,15 +29,17 @@ def tile_list_heave_raggedness_scores_kernel(
         lists = ctx.enter_context(tc.tile_pool(name="lists", bufs=1))
         keep = ctx.enter_context(tc.tile_pool(name="keep", bufs=1))
         ring = ctx.enter_context(tc.tile_pool(name="ring", bufs=5))
-        work = ctx.enter_context(tc.tile_pool(name="work", bufs=3))
         psum = ctx.enter_context(tc.psum_pool(name="psum", bufs=8))
+
+        def kept(shape, dtype, name, tag=None):
+            return keep.tile(shape, dtype, tag=tag or name, name=name, align_bytes=64)
 
         offs_t = lists.tile([P, S // 16], U16, name="offs_t")
         pos1_t = lists.tile([P, NP // 16], U16, name="pos1_t")
         pos2_t = lists.tile([P, NP // 16], U16, name="pos2_t")
         nc.sync.dma_start(offs_t[:], offs)
 
-        sw = ring.tile([P, T], U8, tag="ring", name="sw", align_bytes=64)
+        sw = kept([P, T], U8, "sw", "vw0")
         nc.vector.memset(sw[:].bitcast(I32), 0)
         by_r = tab_scales.rearrange("a (g r) t -> r g a t", r=2)
         for r in range(2):
@@ -47,199 +48,207 @@ def tile_list_heave_raggedness_scores_kernel(
 
         nc.sync.dma_start(pos1_t[:], pos1)
         nc.sync.dma_start(pos2_t[:], pos2)
-        warm_in = keep.tile([P, 8], F32, name="warm_in")
-        warm_out = keep.tile([P, 8], F32, name="warm_out")
+        warm_in = kept([P, 8], F32, "warm_in")
+        warm_out = kept([P, 8], F32, "warm_out")
         nc.gpsimd.memset(warm_in[:], 0.0)
         nc.scalar.activation(warm_out[:], warm_in[:], ACT.Tanh)
 
-        gain_t = keep.tile([P, 2, 4], F32, name="gain_t")
-        w4s = keep.tile([P, 2, N], U8, name="w4s", align_bytes=64)
-        nc.gpsimd.dma_start(gain_t[:], gain.rearrange("(b p t) -> p b t", b=2, t=4))
+        gains = [kept([P, 4], F32, "gain0"), kept([P, 4], F32, "gain1")]
+        w4s = kept([P, 2, N], U8, "w4s")
+        with nc.allow_non_contiguous_dma(reason="one gain a partition"):
+            nc.gpsimd.dma_start(gains[0][:], gain[0:512].rearrange("(c p) -> p c", p=P))
+        nc.gpsimd.dma_start(gains[1][:], gain[512:1024].rearrange("(p t) -> p t", t=4))
         nc.gpsimd.memset(w4s[:].rearrange("p a n -> p (a n)").bitcast(I32), 0)
         w4s_by_r = w4_scales.rearrange("a (q r) n -> r q a n", r=4)
         for r in range(4):
             nc.gpsimd.dma_start(w4s[r:P:32, :, :].bitcast(I32), w4s_by_r[r].bitcast(I32))
 
+        def staged(shape, dtype, name, tag=None):
+            if tag:
+                return kept(shape, dtype, name, tag)
+            return ring.tile(shape, dtype, tag="ring", name=name, align_bytes=64)
+
         def load_tab(a):
-            tab = ring.tile([P, T], U32, tag="ring", name="tab%d" % a, align_bytes=64)
+            tab = staged([P, T], U32, "tab%d" % a, "late" if a == 2 else None)
             nc.sync.dma_start(tab[:].bitcast(I32), tab_words[a].rearrange("p t i -> p (t i)").bitcast(I32))
             return tab
 
-        def load_w1(b, a, c0, width):
-            raw = ring.tile([P, 4, width], F32, tag="ring", name="raw%d%d%d" % (b, a, c0), align_bytes=64)
-            rows = w1[512 * a : 512 * (a + 1), 512 * b + c0 : 512 * b + c0 + width]
+        def load_w1(a, c0, width):
+            raw = staged([P, 4, width], F32, "raw%d_%d" % (a, c0), "late" if (a, c0) == (2, 512) else None)
+            rows = w1[512 * a : 512 * (a + 1), c0 : c0 + width]
             nc.sync.dma_start(raw[:], rows.rearrange("(p j) c -> p j c", j=4))
             return raw
 
-        def cast_w1(engine_copy, grouped, raw, c0, width):
-            dst = grouped[:].rearrange("p (t m j) -> p m j t", t=4, j=4)[:, c0 // 4 : (c0 + width) // 4]
-            engine_copy(dst, raw.rearrange("p j (m t) -> p m j t", t=4))
+        def cast_plain(engine_copy, a, c0, raw):
+            grouped = kept([P, 1024], BF16, "grp%d_%d" % (a, c0))
+            engine_copy(
+                grouped[:].rearrange("p (c i j) -> p c j i", i=4, j=4), raw[:].rearrange("p j (c i) -> p c j i", i=4)
+            )
+            return grouped
+
+        def cast_dealt(engine_copy, grouped, raw, m0, m1):
+            dst = grouped[:].rearrange("p (t m j) -> p m j t", t=4, j=4)[:, m0:m1]
+            engine_copy(dst, raw[:].rearrange("p j (m t) -> p m j t", t=4)[:, m0:m1])
 
         w1q = {}
 
-        def quantize_w1(b, a, grouped, parts):
-            codes = keep.tile([P, 512], U32, name="w1c%d%d" % (b, a), align_bytes=64)
-            scales = keep.tile([P, 512], U8, name="w1s%d%d" % (b, a), align_bytes=64)
-            step = 512 // parts
-            for c in range(0, 512, step):
-                nc.vector.quantize_mx(
-                    out=codes[:, c : c + step].bitcast(FP8X4),
-                    scales=scales[:, c : c + step],
-                    in_=grouped[:, 4 * c : 4 * (c + step)],
-                )
-            w1q[(b, a)] = (codes, scales)
+        def quantize_w1(a, c0, grouped):
+            width = grouped.shape[1] // 4
+            codes = kept([P, width], U32, "w1c%d_%d" % (a, c0))
+            scales = kept([P, width], U8, "w1s%d_%d" % (a, c0))
+            nc.vector.quantize_mx(out=codes[:].bitcast(FP8X4), scales=scales[:], in_=grouped[:])
+            for c in range(0, width, 128):
+                w1q[(a, (c0 + c) // 128)] = (codes[:, c : c + 128], scales[:, c : c + 128])
 
-        def new_grouped(b, a):
-            return keep.tile([P, 2048], BF16, tag="grp%d%d" % (b, a), name="grp%d%d" % (b, a), align_bytes=64)
+        tabs = [load_tab(0), load_tab(1)]
+        early = [load_w1(0, 0, 256), load_w1(1, 0, 256)]
+        tabs.append(load_tab(2))
+        early.append(load_w1(2, 0, 256))
 
-        tabs = [load_tab(0)]
-        raw00 = load_w1(0, 0, 0, 512)
-        tabs.extend([load_tab(1), load_tab(2)])
-        g00, g01, g02 = new_grouped(0, 0), new_grouped(0, 1), new_grouped(0, 2)
-        cast_w1(nc.scalar.copy, g00, raw00[:], 0, 512)
+        sg = kept([P, S], U8, "sg")
+        sf = kept([P, S], U8, "sf")
+        nc.vector.tensor_copy(sg[:], sw[:].indirect(offs_t[:]))
+        nc.vector.tensor_copy(sf[:].bitcast(I32), sg[:].bitcast(I32))
+        for r in range(2):
+            nc.scalar.dma_start(
+                sf[2 + r : 2 + r + 109 : 4, :].bitcast(I32), sg[16 + r : 16 + r + 109 : 4, :].bitcast(I32)
+            )
 
-        vw = []
-        sg = keep.tile([P, S], U8, name="sg", align_bytes=64)
-        sf = keep.tile([P, S], U8, name="sf", align_bytes=64)
-        for a in range(3):
-            v = keep.tile([P, S], U32, tag="vw%d" % a, name="vw%d" % a, align_bytes=64)
-            if a == 0:
-                nc.vector.tensor_copy(sg[:], sw[:].indirect(offs_t[:]))
-                nc.vector.tensor_copy(sf[:].bitcast(I32), sg[:].bitcast(I32))
-                for r in range(2):
-                    nc.sync.dma_start(
-                        sf[2 + r : 2 + r + 109 : 4, :].bitcast(I32), sg[16 + r : 16 + r + 109 : 4, :].bitcast(I32)
-                    )
-            nc.vector.tensor_copy(v[:], tabs[a][:].indirect(offs_t[:]))
-            vw.append(v)
-            if a == 1:
-                quantize_w1(0, 0, g00, 1)
-
-        raw01 = load_w1(0, 1, 0, 512)
-        raw02 = [load_w1(0, 2, c0, 256) for c0 in (0, 256)]
-        raw1 = [load_w1(1, a, 0, 512) for a in range(3)]
+        later = [load_w1(a, 256, 256) for a in range(3)]
+        raw1 = [load_w1(a, 512, 512) for a in range(3)]
         w4w = ring.tile([P, 2, 2 * N], U8, tag="ring", name="w4w", align_bytes=64)
         nc.sync.dma_start(w4w[:].bitcast(I32), w4_words.rearrange("a p n -> p a n").bitcast(I32))
-
         bias_t = ring.tile([P, 6], F32, tag="ring", name="bias_t", align_bytes=64)
         with nc.allow_non_contiguous_dma(reason="one bias value a partition"):
             nc.sync.dma_start(bias_t[:], bias.rearrange("(c p) -> p c", p=P))
 
-        cast_w1(nc.scalar.copy, g01, raw01[:, :, 0:256], 0, 256)
-        cast_w1(nc.vector.tensor_copy, g01, raw01[:, :, 256:512], 256, 256)
-        cast_w1(nc.scalar.copy, g02, raw02[0][:], 0, 256)
-        quantize_w1(0, 1, g01, 1)
-        cast_w1(nc.vector.tensor_copy, g02, raw02[1][:], 256, 256)
-        quantize_w1(0, 2, g02, 2)
+        g_early = [cast_plain(nc.scalar.copy, a, 0, early[a]) for a in range(3)]
+        vw = [kept([P, S], U32, "vw%d" % a) for a in range(3)]
+        nc.vector.tensor_copy(vw[0][:], tabs[0][:].indirect(offs_t[:]))
+        nc.vector.tensor_copy(vw[1][:], tabs[1][:].indirect(offs_t[:]))
+        quantize_w1(0, 0, g_early[0])
+        for half in range(2):
+            nc.vector.tensor_copy(
+                vw[2][:, 512 * half : 512 * (half + 1)], tabs[2][:].indirect(offs_t[:, 32 * half : 32 * (half + 1)])
+            )
+            quantize_w1(1 + half, 0, g_early[1 + half])
 
         banks = {}
 
-        def first_product(b, a, t, last):
-            codes, scales = w1q[(b, a)]
-            for half in range(2):
-                if a == 0:
-                    banks[(b, t, half)] = psum.tile([P, 512], F32, tag="bank", name="hb%d%d%d" % (b, t, half))
-                cols = slice(512 * half, 512 * (half + 1))
-                nc.tensor.matmul_mx(
-                    out=banks[(b, t, half)][:],
-                    lhsT=codes[:, 128 * t : 128 * (t + 1)].bitcast(FP8X4),
-                    lhsT_scale=scales[:, 128 * t : 128 * (t + 1)],
-                    rhs=vw[a][:, cols].bitcast(FP8X4),
-                    rhs_scale=sf[PLANE[a] : P, cols],
-                    start=(a == 0),
-                    stop=(a == last),
-                )
+        def first_product(tile, order):
+            for a in order:
+                codes, scales = w1q[(a, tile)]
+                for half in range(2):
+                    if a == order[0]:
+                        banks[(tile, half)] = psum.tile([P, 512], F32, tag="bank", name="hb%d%d" % (tile, half))
+                    cols = slice(512 * half, 512 * (half + 1))
+                    nc.tensor.matmul_mx(
+                        out=banks[(tile, half)][:],
+                        lhsT=codes.bitcast(FP8X4),
+                        lhsT_scale=scales,
+                        rhs=vw[a][:, cols].bitcast(FP8X4),
+                        rhs_scale=sf[PLANE[a] : P, cols],
+                        start=(a == order[0]),
+                        stop=(a == order[-1]),
+                    )
 
         h = {}
 
-        def evacuate(b, t):
-            h[(b, t)] = keep.tile([P, S], F32, name="h%d%d" % (b, t))
+        def evacuate(tile):
+            h[tile] = kept([P, S], F32, "h%d" % tile)
+            factor = gains[tile // 4][:, tile % 4 : tile % 4 + 1]
             for half in range(2):
-                dst = h[(b, t)][:, 512 * half : 512 * (half + 1)]
-                if (b, t, half) == (0, 0, 1):
-                    nc.vector.tensor_scalar(dst, banks[(b, t, half)][:], gain_t[:, b, t : t + 1], None, ALU.mult)
+                dst = h[tile][:, 512 * half : 512 * (half + 1)]
+                if (tile, half) == (0, 1):
+                    nc.vector.tensor_scalar(dst, banks[(tile, half)][:], factor, None, ALU.mult)
                 else:
-                    nc.scalar.activation(dst, banks[(b, t, half)][:], ACT.Copy, scale=gain_t[:, b, t : t + 1])
+                    nc.scalar.activation(dst, banks[(tile, half)][:], ACT.Copy, scale=factor)
 
-        def clock(src, name):
-            probe = keep.tile([P, 1], F32, name=name)
-            nc.gpsimd.tensor_copy(probe[:], src)
-
-        def pick_second(b, t, m0, width):
-            name = "sec%d%d%d" % (b, t, m0)
-            if (b, t, m0) in REUSE:
-                second = keep.tile([P, width], F32, tag=REUSE[(b, t, m0)], name=name, align_bytes=64)
-            else:
-                second = work.tile([P, width], F32, tag="second", name=name)
-            nc.vector.tensor_copy(second[:], h[(b, t)][:].indirect(pos2_t[:, m0 // 16 : (m0 + width) // 16]))
+        def pick_second(tile, m0, width, tag=None):
+            second = kept([P, width], F32, "sec%d_%d" % (tile, m0), tag)
+            nc.vector.tensor_copy(second[:], h[tile][:].indirect(pos2_t[:, m0 // 16 : (m0 + width) // 16]))
             return second
 
-        def subtract(diff, second, b, t, m0, width):
+        def subtract(dst, second, tile, m0, width):
             nc.vector.tensor_tensor(
-                diff[:, t, :], h[(b, t)][:].indirect(pos1_t[:, m0 // 16 : (m0 + width) // 16]), second[:], ALU.subtract
+                dst, h[tile][:].indirect(pos1_t[:, m0 // 16 : (m0 + width) // 16]), second[:], ALU.subtract
             )
 
-        def quantize_rag(diff, b, m0, width):
-            tag = "vw1" if b == 0 else "rb%d" % m0
-            rb = keep.tile([P, 4 * width], BF16, tag=tag, name="rb%d%d" % (b, m0), align_bytes=64)
+        def quantize_rag(diff, name, width, tag=None):
+            rb = kept([P, 4 * width], BF16, "rb" + name, tag)
             nc.scalar.activation(
                 rb[:].rearrange("p (c i t) -> p c t i", i=4, t=4),
                 diff[:].rearrange("p t (c i) -> p c t i", i=4),
                 ACT.Abs,
             )
-            codes = keep.tile([P, width], U32, name="rc%d%d" % (b, m0), align_bytes=64)
-            scales = keep.tile([P, width], U8, name="rs%d%d" % (b, m0), align_bytes=64)
+            codes = kept([P, width], U32, "rc" + name)
+            scales = kept([P, width], U8, "rs" + name)
             nc.vector.quantize_mx(out=codes[:].bitcast(FP8X4), scales=scales[:], in_=rb[:])
             return codes, scales
 
-        for t in range(4):
-            for a in range(3):
-                first_product(0, a, t, 2)
+        diff0 = kept([P, 4, NP], F32, "diff0", "late")
 
-        g1 = [new_grouped(1, a) for a in range(3)]
-        diff0 = keep.tile([P, 4, NP], F32, name="diff0")
-        for t in range(3):
-            evacuate(0, t)
-        cast_w1(nc.scalar.copy, g1[0], raw1[0][:], 0, 512)
-        cast_w1(nc.scalar.copy, g1[1], raw1[1][:], 0, 512)
-        evacuate(0, 3)
-        clock(h[(0, 0)][:, 0:1], "clk1")
-        seconds = [pick_second(0, t, 0, NP) for t in (0, 1)]
-        for t in range(2):
-            subtract(diff0, seconds[t], 0, t, 0, NP)
-        cast_w1(nc.vector.tensor_copy, g1[2], raw1[2][:], 0, 512)
-        quantize_w1(1, 0, g1[0], 1)
-        quantize_w1(1, 2, g1[2], 1)
-        second = pick_second(0, 2, 0, NP)
-        quantize_w1(1, 1, g1[1], 1)
-        subtract(diff0, second, 0, 2, 0, NP)
-        second = pick_second(0, 3, 0, NP)
-        subtract(diff0, second, 0, 3, 0, NP)
-        for t in range(4):
-            for a in (0, 2, 1):
-                first_product(1, a, t, 1)
-            evacuate(1, t)
+        def subtract_and_deal(tile, second, tag=None):
+            rows = kept([P, NP], F32, "rows%d" % tile, tag)
+            subtract(rows[:], second, tile, 0, NP)
+            nc.sync.dma_start(diff0[32 * tile : 32 * (tile + 1), :, :], rows[:])
 
-        clock(h[(1, 0)][:, 1023:1024], "clk2")
+        first_product(0, (0, 1, 2))
+        first_product(1, (0, 1, 2))
+        evacuate(0)
+        g_later = [cast_plain(nc.scalar.copy, a, 256, later[a]) for a in range(3)]
+        evacuate(1)
+        second = pick_second(0, 0, NP)
+        for a in range(3):
+            quantize_w1(a, 256, g_later[a])
+        subtract_and_deal(0, second, "grp2_256")
+        first_product(2, (0, 1, 2))
+        first_product(3, (0, 1, 2))
+        evacuate(2)
+        g1 = [kept([P, 2048], BF16, "grp%d_512" % a) for a in range(3)]
+        for m0 in (0, 64):
+            cast_dealt(nc.scalar.copy, g1[0], raw1[0], m0, m0 + 64)
+        evacuate(3)
+        cast_dealt(nc.scalar.copy, g1[1], raw1[1], 0, 128)
+        cast_dealt(nc.scalar.copy, g1[2], raw1[2], 0, 64)
+        seconds = [pick_second(tile, 0, NP) for tile in (1, 2)]
+        subtract_and_deal(1, seconds[0])
+        subtract_and_deal(2, seconds[1])
+        cast_dealt(nc.vector.tensor_copy, g1[2], raw1[2], 64, 128)
+        quantize_w1(0, 512, g1[0])
+        second = pick_second(3, 0, NP, "grp0_512")
+        quantize_w1(1, 512, g1[1])
+        quantize_w1(2, 512, g1[2])
+        subtract_and_deal(3, second, "grp2_512")
+        for tile in range(4, 8):
+            first_product(tile, (0, 1, 2))
+            evacuate(tile)
+
         out_v = out.rearrange("(c p) m -> p c m", p=P)
         rag = {}
+        held_behind = {
+            (4, 0): "even", (6, 0): "even", (4, 256): "even",
+            (5, 0): "odd", (7, 0): "odd", (5, 256): "odd",
+            (6, 256): "late", (4, 384): "late", (7, 256): "diff1_0", (5, 384): "diff1_0",
+            (6, 384): "rb256", (7, 384): "diff1_256",
+        }
 
         def pick_chunk(m0, width):
-            diff = keep.tile([P, 4, width], F32, name="diff1%d" % m0)
-            for pair in range(2):
-                seconds = [pick_second(1, t, m0, width) for t in (2 * pair, 2 * pair + 1)]
-                for u in range(2):
-                    subtract(diff, seconds[u], 1, 2 * pair + u, m0, width)
+            diff = kept([P, 4, width], F32, "diff1_%d" % m0)
+            for pair in ((4, 5), (6, 7)):
+                seconds = [pick_second(tile, m0, width, held_behind.get((tile, m0))) for tile in pair]
+                for tile, second in zip(pair, seconds):
+                    subtract(diff[:, tile - 4, :], second, tile, m0, width)
             if m0 == 0:
-                rag[0] = quantize_rag(diff0, 0, 0, NP)
-            rag[(1, m0)] = quantize_rag(diff, 1, m0, width)
+                rag["first"] = quantize_rag(diff0, "first", NP, "vw2")
+            rag[m0] = quantize_rag(diff, "%d" % m0, width, "late" if m0 == 0 else None)
 
         def finish_chunk(m0, width):
-            y = keep.tile([P, 6, width], F32, name="y%d" % m0)
+            y = kept([P, 6, width], F32, "y%d" % m0)
             for c in range(6):
                 bank = psum.tile([P, 512], F32, tag="bank", name="yb%d%d" % (m0, c))
                 for s0 in range(0, width, 128):
-                    for a, (codes, scales, c0) in enumerate((rag[0] + (m0 + s0,), rag[(1, m0)] + (s0,))):
+                    for a, (codes, scales, c0) in enumerate((rag["first"] + (m0 + s0,), rag[m0] + (s0,))):
                         nc.tensor.matmul_mx(
                             out=bank[:, s0 : s0 + 128],
                             lhsT=w4w[:, a, 256 * c : 256 * (c + 1)].bitcast(FP4X4),

@@ -166,13 +166,19 @@ def tile_list_heave_raggedness_scores_kernel(
 
         def pick_second(tile, m0, width, tag=None):
             second = kept([P, width], F32, "sec%d_%d" % (tile, m0), tag)
-            nc.vector.tensor_copy(second[:], h[tile][:].indirect(pos2_t[:, m0 // 16 : (m0 + width) // 16]))
+            step = width // 2 if m0 == 0 else width
+            for s0 in range(0, width, step):
+                picks = pos2_t[:, (m0 + s0) // 16 : (m0 + s0 + step) // 16]
+                nc.vector.tensor_copy(second[:, s0 : s0 + step], h[tile][:].indirect(picks))
             return second
 
         def subtract(dst, second, tile, m0, width):
-            nc.vector.tensor_tensor(
-                dst, h[tile][:].indirect(pos1_t[:, m0 // 16 : (m0 + width) // 16]), second[:], ALU.subtract
-            )
+            step = width // 2 if m0 == 0 else width
+            for s0 in range(0, width, step):
+                picks = pos1_t[:, (m0 + s0) // 16 : (m0 + s0 + step) // 16]
+                nc.vector.tensor_tensor(
+                    dst[:, s0 : s0 + step], h[tile][:].indirect(picks), second[:, s0 : s0 + step], ALU.subtract
+                )
 
         def quantize_rag(diff, name, width, tag=None):
             rb = kept([P, 4 * width], BF16, "rb" + name, tag)
@@ -235,7 +241,7 @@ def tile_list_heave_raggedness_scores_kernel(
 
         def pick_chunk(m0, width):
             diff = kept([P, 4, width], F32, "diff1_%d" % m0)
-            for pair in ((4, 5), (6, 7)):
+            for pair in ((4, 5), (6, 7) if m0 == 0 else (7, 6)):
                 seconds = [pick_second(tile, m0, width, held_behind.get((tile, m0))) for tile in pair]
                 for tile, second in zip(pair, seconds):
                     subtract(diff[:, tile - 4, :], second, tile, m0, width)
@@ -243,27 +249,37 @@ def tile_list_heave_raggedness_scores_kernel(
                 rag["first"] = quantize_rag(diff0, "first", NP, "vw2")
             rag[m0] = quantize_rag(diff, "%d" % m0, width, "late" if m0 == 0 else None)
 
-        def finish_chunk(m0, width):
+        def second_product(dst, c, a, codes, scales, c0):
+            nc.tensor.matmul_mx(
+                out=dst,
+                lhsT=w4w[:, a, 256 * c : 256 * (c + 1)].bitcast(FP4X4),
+                lhsT_scale=w4s[:, a, 128 * c : 128 * (c + 1)],
+                rhs=codes[:, c0 : c0 + 128].bitcast(FP8X4),
+                rhs_scale=scales[:, c0 : c0 + 128],
+                start=(a == 0),
+                stop=(a == 1),
+            )
+
+        def finish_chunk(m0, width, per_bank):
             y = kept([P, 6, width], F32, "y%d" % m0)
-            for c in range(6):
-                bank = psum.tile([P, 512], F32, tag="bank", name="yb%d%d" % (m0, c))
-                for s0 in range(0, width, 128):
-                    for a, (codes, scales, c0) in enumerate((rag["first"] + (m0 + s0,), rag[m0] + (s0,))):
-                        nc.tensor.matmul_mx(
-                            out=bank[:, s0 : s0 + 128],
-                            lhsT=w4w[:, a, 256 * c : 256 * (c + 1)].bitcast(FP4X4),
-                            lhsT_scale=w4s[:, a, 128 * c : 128 * (c + 1)],
-                            rhs=codes[:, c0 : c0 + 128].bitcast(FP8X4),
-                            rhs_scale=scales[:, c0 : c0 + 128],
-                            start=(a == 0),
-                            stop=(a == 1),
-                        )
-                nc.scalar.activation(y[:, c, :], bank[:, 0:width], ACT.Tanh, bias=bias_t[:, c : c + 1])
-            for c0 in (0, 3):
-                nc.sync.dma_start(out_v[:, c0 : c0 + 3, m0 : m0 + width], y[:, c0 : c0 + 3, :])
+            for c0 in range(0, 6, per_bank):
+                bank = psum.tile([P, 512], F32, tag="bank", name="yb%d%d" % (m0, c0))
+                for u in range(per_bank):
+                    for s0 in range(0, width, 128):
+                        dst = bank[:, u * width + s0 : u * width + s0 + 128]
+                        second_product(dst, c0 + u, 0, *rag["first"], m0 + s0)
+                        second_product(dst, c0 + u, 1, *rag[m0], s0)
+                for u in range(per_bank):
+                    c = c0 + u
+                    nc.scalar.activation(
+                        y[:, c, :], bank[:, u * width : (u + 1) * width], ACT.Tanh, bias=bias_t[:, c : c + 1]
+                    )
+            for queue, c0, c1 in ((nc.sync, 0, 4), (nc.scalar if per_bank == 1 else nc.sync, 4, 6)):
+                queue.dma_start(out_v[:, c0:c1, m0 : m0 + width], y[:, c0:c1, :])
 
         pick_chunk(*CHUNKS[0])
-        for k in range(1, len(CHUNKS)):
-            pick_chunk(*CHUNKS[k])
-            finish_chunk(*CHUNKS[k - 1])
-        finish_chunk(*CHUNKS[-1])
+        pick_chunk(*CHUNKS[1])
+        finish_chunk(*CHUNKS[0], 2)
+        pick_chunk(*CHUNKS[2])
+        finish_chunk(*CHUNKS[1], 3)
+        finish_chunk(*CHUNKS[2], 1)

from contextlib import ExitStack

import concourse.mybir as mybir

K, T, S, NP, H, N = 1536, 2048, 1024, 512, 1024, 768
FLOPS = 2 * K * H * S + 2 * H * N * NP

F32 = mybir.dt.float32
BF16 = mybir.dt.bfloat16
I32 = mybir.dt.int32
U32 = mybir.dt.uint32
U16 = mybir.dt.uint16
U8 = mybir.dt.uint8
FP8X4 = mybir.dt.float8_e4m3fn_x4
FP4X4 = mybir.dt.float4_e2m1fn_x4
ACT = mybir.ActivationFunctionType
ALU = mybir.AluOpType

P = 128
PLANE = (0, 8, 4)
CHUNKS = ((0, 256), (256, 128), (384, 128))


def tile_list_heave_raggedness_scores_kernel(
    tc, tab_words, tab_scales, offs, pos1, pos2, w1, gain, w4_words, w4_scales, bias, out
):
    nc = tc.nc
    with ExitStack() as ctx:
        lists = ctx.enter_context(tc.tile_pool(name="lists", bufs=1))
        keep = ctx.enter_context(tc.tile_pool(name="keep", bufs=1))
        ring = ctx.enter_context(tc.tile_pool(name="ring", bufs=5))
        psum = ctx.enter_context(tc.psum_pool(name="psum", bufs=8))

        def kept(shape, dtype, name, tag=None):
            return keep.tile(shape, dtype, tag=tag or name, name=name, align_bytes=64)

        offs_t = lists.tile([P, S // 16], U16, name="offs_t")
        pos1_t = lists.tile([P, NP // 16], U16, name="pos1_t")
        pos2_t = lists.tile([P, NP // 16], U16, name="pos2_t")
        nc.sync.dma_start(offs_t[:], offs)

        sw = kept([P, T], U8, "sw", "vw0")
        nc.vector.memset(sw[:].bitcast(I32), 0)
        by_r = tab_scales.rearrange("a (g r) t -> r g a t", r=2)
        for r in range(2):
            nc.sync.dma_start(sw[r:P:8, :].bitcast(I32), by_r[r, :, 0:2, :].bitcast(I32))
            nc.sync.dma_start(sw[4 + r : P : 16, :].bitcast(I32), by_r[r, :, 2, :].bitcast(I32))

        nc.sync.dma_start(pos1_t[:], pos1)
        nc.sync.dma_start(pos2_t[:], pos2)
        warm_in = kept([P, 8], F32, "warm_in")
        warm_out = kept([P, 8], F32, "warm_out")
        nc.gpsimd.memset(warm_in[:], 0.0)
        nc.scalar.activation(warm_out[:], warm_in[:], ACT.Tanh)

        gains = [kept([P, 4], F32, "gain0"), kept([P, 4], F32, "gain1")]
        w4s = kept([P, 2, N], U8, "w4s")
        with nc.allow_non_contiguous_dma(reason="one gain a partition"):
            nc.gpsimd.dma_start(gains[0][:], gain[0:512].rearrange("(c p) -> p c", p=P))
        nc.gpsimd.dma_start(gains[1][:], gain[512:1024].rearrange("(p t) -> p t", t=4))
        nc.gpsimd.memset(w4s[:].rearrange("p a n -> p (a n)").bitcast(I32), 0)
        w4s_by_r = w4_scales.rearrange("a (q r) n -> r q a n", r=4)
        for r in range(4):
            nc.gpsimd.dma_start(w4s[r:P:32, :, :].bitcast(I32), w4s_by_r[r].bitcast(I32))

        def staged(shape, dtype, name, tag=None):
            if tag:
                return kept(shape, dtype, name, tag)
            return ring.tile(shape, dtype, tag="ring", name=name, align_bytes=64)

        def load_tab(a):
            tab = staged([P, T], U32, "tab%d" % a, "late" if a == 2 else None)
            nc.sync.dma_start(tab[:].bitcast(I32), tab_words[a].rearrange("p t i -> p (t i)").bitcast(I32))
            return tab

        def load_w1(a, c0, width):
            raw = staged([P, 4, width], F32, "raw%d_%d" % (a, c0), "late" if (a, c0) == (2, 512) else None)
            rows = w1[512 * a : 512 * (a + 1), c0 : c0 + width]
            nc.sync.dma_start(raw[:], rows.rearrange("(p j) c -> p j c", j=4))
            return raw

        def cast_plain(engine_copy, a, c0, raw):
            grouped = kept([P, 1024], BF16, "grp%d_%d" % (a, c0))
            engine_copy(
                grouped[:].rearrange("p (c i j) -> p c j i", i=4, j=4), raw[:].rearrange("p j (c i) -> p c j i", i=4)
            )
            return grouped

        def cast_dealt(engine_copy, grouped, raw, m0, m1):
            dst = grouped[:].rearrange("p (t m j) -> p m j t", t=4, j=4)[:, m0:m1]
            engine_copy(dst, raw[:].rearrange("p j (m t) -> p m j t", t=4)[:, m0:m1])

        w1q = {}

        def quantize_w1(a, c0, grouped):
            width = grouped.shape[1] // 4
            codes = kept([P, width], U32, "w1c%d_%d" % (a, c0))
            scales = kept([P, width], U8, "w1s%d_%d" % (a, c0))
            nc.vector.quantize_mx(out=codes[:].bitcast(FP8X4), scales=scales[:], in_=grouped[:])
            for c in range(0, width, 128):
                w1q[(a, (c0 + c) // 128)] = (codes[:, c : c + 128], scales[:, c : c + 128])

        tabs = [load_tab(0), load_tab(1)]
        early = [load_w1(0, 0, 256), load_w1(1, 0, 256)]
        tabs.append(load_tab(2))
        early.append(load_w1(2, 0, 256))

        sg = kept([P, S], U8, "sg")
        sf = kept([P, S], U8, "sf")
        nc.vector.tensor_copy(sg[:], sw[:].indirect(offs_t[:]))
        nc.vector.tensor_copy(sf[:].bitcast(I32), sg[:].bitcast(I32))
        for r in range(2):
            nc.scalar.dma_start(
                sf[2 + r : 2 + r + 109 : 4, :].bitcast(I32), sg[16 + r : 16 + r + 109 : 4, :].bitcast(I32)
            )

        later = [load_w1(a, 256, 256) for a in range(3)]
        raw1 = [load_w1(a, 512, 512) for a in range(3)]
        w4w = ring.tile([P, 2, 2 * N], U8, tag="ring", name="w4w", align_bytes=64)
        nc.sync.dma_start(w4w[:].bitcast(I32), w4_words.rearrange("a p n -> p a n").bitcast(I32))
        bias_t = ring.tile([P, 6], F32, tag="ring", name="bias_t", align_bytes=64)
        with nc.allow_non_contiguous_dma(reason="one bias value a partition"):
            nc.sync.dma_start(bias_t[:], bias.rearrange("(c p) -> p c", p=P))

        g_early = [cast_plain(nc.scalar.copy, a, 0, early[a]) for a in range(3)]
        vw = [kept([P, S], U32, "vw%d" % a) for a in range(3)]
        nc.vector.tensor_copy(vw[0][:], tabs[0][:].indirect(offs_t[:]))
        nc.vector.tensor_copy(vw[1][:], tabs[1][:].indirect(offs_t[:]))
        quantize_w1(0, 0, g_early[0])
        for half in range(2):
            nc.vector.tensor_copy(
                vw[2][:, 512 * half : 512 * (half + 1)], tabs[2][:].indirect(offs_t[:, 32 * half : 32 * (half + 1)])
            )
            quantize_w1(1 + half, 0, g_early[1 + half])

        banks = {}

        def first_product(tile, order):
            for a in order:
                codes, scales = w1q[(a, tile)]
                for half in range(2):
                    if a == order[0]:
                        banks[(tile, half)] = psum.tile([P, 512], F32, tag="bank", name="hb%d%d" % (tile, half))
                    cols = slice(512 * half, 512 * (half + 1))
                    nc.tensor.matmul_mx(
                        out=banks[(tile, half)][:],
                        lhsT=codes.bitcast(FP8X4),
                        lhsT_scale=scales,
                        rhs=vw[a][:, cols].bitcast(FP8X4),
                        rhs_scale=sf[PLANE[a] : P, cols],
                        start=(a == order[0]),
                        stop=(a == order[-1]),
                    )

        h = {}

        def evacuate(tile):
            h[tile] = kept([P, S], F32, "h%d" % tile)
            factor = gains[tile // 4][:, tile % 4 : tile % 4 + 1]
            for half in range(2):
                dst = h[tile][:, 512 * half : 512 * (half + 1)]
                if (tile, half) == (0, 1):
                    nc.vector.tensor_scalar(dst, banks[(tile, half)][:], factor, None, ALU.mult)
                else:
                    nc.scalar.activation(dst, banks[(tile, half)][:], ACT.Copy, scale=factor)

        def pick_second(tile, m0, width, tag=None):
            second = kept([P, width], F32, "sec%d_%d" % (tile, m0), tag)
            step = width // 2 if m0 == 0 else width
            for s0 in range(0, width, step):
                picks = pos2_t[:, (m0 + s0) // 16 : (m0 + s0 + step) // 16]
                nc.vector.tensor_copy(second[:, s0 : s0 + step], h[tile][:].indirect(picks))
            return second

        def subtract(dst, second, tile, m0, width):
            step = width // 2 if m0 == 0 else width
            for s0 in range(0, width, step):
                picks = pos1_t[:, (m0 + s0) // 16 : (m0 + s0 + step) // 16]
                nc.vector.tensor_tensor(
                    dst[:, s0 : s0 + step], h[tile][:].indirect(picks), second[:, s0 : s0 + step], ALU.subtract
                )

        def quantize_rag(diff, name, width, tag=None):
            rb = kept([P, 4 * width], BF16, "rb" + name, tag)
            nc.scalar.activation(
                rb[:].rearrange("p (c i t) -> p c t i", i=4, t=4),
                diff[:].rearrange("p t (c i) -> p c t i", i=4),
                ACT.Abs,
            )
            codes = kept([P, width], U32, "rc" + name)
            scales = kept([P, width], U8, "rs" + name)
            nc.vector.quantize_mx(out=codes[:].bitcast(FP8X4), scales=scales[:], in_=rb[:])
            return codes, scales

        diff0 = kept([P, 4, NP], F32, "diff0", "late")

        def subtract_and_deal(tile, second, tag=None):
            rows = kept([P, NP], F32, "rows%d" % tile, tag)
            subtract(rows[:], second, tile, 0, NP)
            nc.sync.dma_start(diff0[32 * tile : 32 * (tile + 1), :, :], rows[:])

        first_product(0, (0, 1, 2))
        first_product(1, (0, 1, 2))
        evacuate(0)
        g_later = [cast_plain(nc.scalar.copy, a, 256, later[a]) for a in range(3)]
        evacuate(1)
        second = pick_second(0, 0, NP)
        for a in range(3):
            quantize_w1(a, 256, g_later[a])
        subtract_and_deal(0, second, "grp2_256")
        first_product(2, (0, 1, 2))
        first_product(3, (0, 1, 2))
        evacuate(2)
        g1 = [kept([P, 2048], BF16, "grp%d_512" % a) for a in range(3)]
        for m0 in (0, 64):
            cast_dealt(nc.scalar.copy, g1[0], raw1[0], m0, m0 + 64)
        evacuate(3)
        cast_dealt(nc.scalar.copy, g1[1], raw1[1], 0, 128)
        cast_dealt(nc.scalar.copy, g1[2], raw1[2], 0, 64)
        seconds = [pick_second(tile, 0, NP) for tile in (1, 2)]
        subtract_and_deal(1, seconds[0])
        subtract_and_deal(2, seconds[1])
        cast_dealt(nc.vector.tensor_copy, g1[2], raw1[2], 64, 128)
        quantize_w1(0, 512, g1[0])
        second = pick_second(3, 0, NP, "grp0_512")
        quantize_w1(1, 512, g1[1])
        quantize_w1(2, 512, g1[2])
        subtract_and_deal(3, second, "grp2_512")
        for tile in range(4, 8):
            first_product(tile, (0, 1, 2))
            evacuate(tile)

        out_v = out.rearrange("(c p) m -> p c m", p=P)
        rag = {}
        held_behind = {
            (4, 0): "even", (6, 0): "even", (4, 256): "even",
            (5, 0): "odd", (7, 0): "odd", (5, 256): "odd",
            (6, 256): "late", (4, 384): "late", (7, 256): "diff1_0", (5, 384): "diff1_0",
            (6, 384): "rb256", (7, 384): "diff1_256",
        }

        def pick_chunk(m0, width):
            diff = kept([P, 4, width], F32, "diff1_%d" % m0)
            for pair in ((4, 5), (6, 7) if m0 == 0 else (7, 6)):
                seconds = [pick_second(tile, m0, width, held_behind.get((tile, m0))) for tile in pair]
                for tile, second in zip(pair, seconds):
                    subtract(diff[:, tile - 4, :], second, tile, m0, width)
            if m0 == 0:
                rag["first"] = quantize_rag(diff0, "first", NP, "vw2")
            rag[m0] = quantize_rag(diff, "%d" % m0, width, "late" if m0 == 0 else None)

        def second_product(dst, c, a, codes, scales, c0):
            nc.tensor.matmul_mx(
                out=dst,
                lhsT=w4w[:, a, 256 * c : 256 * (c + 1)].bitcast(FP4X4),
                lhsT_scale=w4s[:, a, 128 * c : 128 * (c + 1)],
                rhs=codes[:, c0 : c0 + 128].bitcast(FP8X4),
                rhs_scale=scales[:, c0 : c0 + 128],
                start=(a == 0),
                stop=(a == 1),
            )

        def finish_chunk(m0, width, per_bank):
            y = kept([P, 6, width], F32, "y%d" % m0)
            for c0 in range(0, 6, per_bank):
                bank = psum.tile([P, 512], F32, tag="bank", name="yb%d%d" % (m0, c0))
                for u in range(per_bank):
                    for s0 in range(0, width, 128):
                        dst = bank[:, u * width + s0 : u * width + s0 + 128]
                        second_product(dst, c0 + u, 0, *rag["first"], m0 + s0)
                        second_product(dst, c0 + u, 1, *rag[m0], s0)
                for u in range(per_bank):
                    c = c0 + u
                    nc.scalar.activation(
                        y[:, c, :], bank[:, u * width : (u + 1) * width], ACT.Tanh, bias=bias_t[:, c : c + 1]
                    )
            for queue, c0, c1 in ((nc.sync, 0, 4), (nc.scalar if per_bank == 1 else nc.sync, 4, 6)):
                queue.dma_start(out_v[:, c0:c1, m0 : m0 + width], y[:, c0:c1, :])

        pick_chunk(*CHUNKS[0])
        pick_chunk(*CHUNKS[1])
        finish_chunk(*CHUNKS[0], 2)
        pick_chunk(*CHUNKS[2])
        finish_chunk(*CHUNKS[1], 3)
        finish_chunk(*CHUNKS[2], 1)
